import numpy as np
CORES = [50,55,434,439,178,183,306,311]
N = 8
GR, GC, W, CW, TIMES = 4, 2, 128, 2, 1
def setup_inputs(rng):
    return {"x": rng.standard_normal((N, 128, W), dtype=np.float32)}
def reference(x):
    X = x.astype(np.float64).reshape(GR, GC, 128, W)
    g = np.concatenate([np.concatenate(list(X[i]), axis=1) for i in range(GR)], axis=0)
    for _ in range(TIMES):
        g = CW * g + np.roll(g, 1, 0) + np.roll(g, -1, 0) + np.roll(g, 1, 1) + np.roll(g, -1, 1)
    return {"y": np.stack([g[128 * (r // GC):128 * (r // GC) + 128, W * (r % GC):W * (r % GC) + W] for r in range(N)]).astype(np.float32 if x.dtype != np.float64 else np.float64)}

@@ -1,0 +1,141 @@
+from concourse.mybir import AluOpType
+
+GR, GC, P, W = 4, 2, 128, 128
+HOSTS = 4
+
+SCRATCH = {
+    "sb":  ("dram", [2, P, 1], "float32"),
+    "lnd": ("dram", [2, P, 1], "float32"),
+    "rb":  ("dram", [P, 1], "float32"),
+    "w":   ("sbuf", [P, W + 2], "float32"),
+    "xu":  ("sbuf", [P, W], "float32"),
+    "xd":  ("sbuf", [P, W], "float32"),
+    "q":   ("sbuf", [P, W], "float32"),
+    "s":   ("sbuf", [P, W], "float32"),
+    "cb":  ("sbuf", [P, 2], "float32"),
+}
+SEMAPHORES = ["ldr", "ldw", "ldt", "ldu", "ldd", "vs", "carr", "arr", "rarr", "sent", "strow", "stmain", "acc"]
+
+_PLAN = {}
+
+
+def _engines(topo, src, dst, n, skip=0):
+    m = topo.mask(src, dst)
+    bits = [b for b in range(m.bit_length()) if (m >> b) & 1]
+    if n is None:
+        n = len(bits)
+    sel = bits[skip:skip + n]
+    return sum(1 << b for b in sel), len(sel)
+
+
+def _plan(T, topo):
+    if "m" in _PLAN:
+        return _PLAN["m"]
+    cores = list(T.cores)
+    world = range(HOSTS * topo.CORES_PER_HOST)
+    used = set()
+    msgs = []
+    for r, s in enumerate(cores):
+        gr, gc = divmod(r, GC)
+        for step, sslot, dslot in ((-1, 0, 1), (1, 1, 0)):
+            d = cores[((gr + step) % GR) * GC + gc]
+            relay = None
+            if not topo.may_write(s, d):
+                for c in world:
+                    if (c not in cores and c not in used and topo.chip(c) == topo.chip(s) == topo.chip(d)
+                            and topo.die(c) == topo.die(s) and topo.same_plane(s, c)
+                            and topo.may_write(s, c) and topo.may_write(c, d)):
+                        relay = c
+                        break
+                used.add(relay)
+            msgs.append((s, d, sslot, dslot, relay))
+    _PLAN["m"] = msgs
+    return msgs
+
+
+def rank_program(g, core, T, topo):
+    msgs = _plan(T, topo)
+    sem = T.sem
+    rank = T.rank_of(core)
+
+    if rank is None:
+        for (s, d, sslot, dslot, relay) in msgs:
+            if relay == core:
+                _, n_in = _engines(topo, s, core, 1)
+                m, n = _engines(topo, core, d, 1)
+                rid, pid = topo.addr(d, core)
+                g.wait_ge(sem.rarr, n_in)
+                g.remote_dma(T.lnd[dslot], T.rb[:], sem.arr, sem.sent, pid, rid, m)
+                g.wait_ge(sem.sent, n)
+        return
+
+    add = AluOpType.add
+    v = g.vector
+    peer = T.cores[rank ^ 1] if GC == 2 else None
+    mine = [mm for mm in msgs if mm[0] == core]
+    far = [mm for mm in mine if mm[4] is not None]
+    near = [mm for mm in mine if mm[4] is None]
+
+    g.sync.dma_start(T.sb[:], T.x[0:P:P - 1, :]).then_inc(sem.ldr, 16)
+    g.scalar.dma_start(T.w[:, W:W + 2], T.x[:, 0:2]).then_inc(sem.ldt, 16)
+    g.sync.dma_start(T.w[:, 0:W], T.x[:, :]).then_inc(sem.ldw, 16)
+    g.scalar.dma_start(T.xu[1:P, :], T.x[0:P - 1, :]).then_inc(sem.ldu, 16)
+    g.sync.dma_start(T.xd[0:P - 1, :], T.x[1:P, :]).then_inc(sem.ldd, 16)
+
+    sent = 0
+    g.wait_ge(sem.ldr, 16)
+    for (s, d, sslot, dslot, relay) in far:
+        m, n = _engines(topo, core, relay, 1)
+        rid, pid = topo.addr(relay, core)
+        g.remote_dma(T.rb[:], T.sb[sslot], sem.rarr, sem.sent, pid, rid, m)
+        sent += n
+    g.wait_ge(sem.ldw, 16)
+    g.wait_ge(sem.ldt, 16)
+    m, ncol = _engines(topo, core, peer, None)
+    rid, pid = topo.addr(peer, core)
+    g.remote_dma(T.cb[:, :], T.w[:, W - 1:W + 1], sem.carr, sem.sent, pid, rid, m)
+    sent += ncol
+    for (s, d, sslot, dslot, relay) in near:
+        m, n = _engines(topo, core, d, 1, skip=1)
+        rid, pid = topo.addr(d, core)
+        g.remote_dma(T.lnd[dslot], T.sb[sslot], sem.arr, sem.sent, pid, rid, m)
+        sent += n
+
+    nv = [0]
+
+    def done(inst):
+        inst.then_inc(sem.vs, 1)
+        nv[0] += 1
+
+    def sync_v():
+        v.wait_ge(sem.vs, nv[0])
+
+    done(v.memset(T.xu[0:1, :], 0.0))
+    v.wait_ge(sem.ldw, 16)
+    done(v.tensor_tensor(T.q[:, 0:W - 1], T.w[:, 0:W - 1], T.w[:, 1:W], add))
+    sync_v()
+    done(v.tensor_tensor(T.s[:, 1:W - 1], T.q[:, 0:W - 2], T.q[:, 1:W - 1], add))
+    done(v.tensor_tensor(T.s[:, 0:1], T.q[:, 0:1], T.w[:, 0:1], add))
+    done(v.tensor_tensor(T.s[:, W - 1:W], T.q[:, W - 2:W - 1], T.w[:, W - 1:W], add))
+    v.wait_ge(sem.ldu, 16)
+    v.wait_ge(sem.ldd, 16)
+    done(v.tensor_tensor(T.xu[0:P - 1, :], T.xu[0:P - 1, :], T.xd[0:P - 1, :], add))
+    sync_v()
+    done(v.tensor_tensor(T.s[:, :], T.s[:, :], T.xu[:, :], add))
+    sync_v()
+    v.wait_ge(sem.carr, ncol)
+    done(v.tensor_tensor(T.s[:, 0:1], T.s[:, 0:1], T.cb[:, 0:1], add))
+    done(v.tensor_tensor(T.s[:, W - 1:W], T.s[:, W - 1:W], T.cb[:, 1:2], add))
+
+    g.sync.wait_ge(sem.vs, nv[0])
+    g.scalar.wait_ge(sem.vs, nv[0])
+    g.sync.dma_start(T.y[0:1, :], T.s[0:1, :]).then_inc(sem.strow, 16)
+    g.scalar.dma_start(T.y[P - 1:P, :], T.s[P - 1:P, :]).then_inc(sem.strow, 16)
+    g.sync.dma_start(T.y[1:P - 1, :], T.s[1:P - 1, :]).then_inc(sem.stmain, 16)
+
+    g.wait_ge(sem.strow, 32)
+    g.wait_ge(sem.arr, 2)
+    g.dma_start(T.y[0:P:P - 1, :], T.lnd[:], accum_op=add).then_inc(sem.acc, 16)
+    g.wait_ge(sem.acc, 16)
+    g.wait_ge(sem.stmain, 16)
+    g.wait_ge(sem.sent, sent)

@@ -2,19 +2,25 @@ from concourse.mybir import AluOpType
 
 GR, GC, P, W = 4, 2, 128, 128
 HOSTS = 4
+BANK = 512
 
 SCRATCH = {
     "sb":  ("dram", [2, P, 1], "float32"),
-    "lnd": ("dram", [2, P, 1], "float32"),
     "rb":  ("dram", [P, 1], "float32"),
+    "hb":  ("sbuf", [P, 8], "float32"),
+    "fc":  ("sbuf", [P, 8], "float32"),
     "w":   ("sbuf", [P, W + 2], "float32"),
     "xu":  ("sbuf", [P, W], "float32"),
     "xd":  ("sbuf", [P, W], "float32"),
     "q":   ("sbuf", [P, W], "float32"),
     "s":   ("sbuf", [P, W], "float32"),
     "cb":  ("sbuf", [P, 2], "float32"),
+    "one": ("sbuf", [P, 4], "float32"),
+    "ev":  ("sbuf", [P, 4], "float32"),
+    "pt":  ("psum", [P, 2 * BANK], "float32"),
 }
-SEMAPHORES = ["ldr", "ldw", "ldt", "ldu", "ldd", "vs", "carr", "arr", "rarr", "sent", "strow", "stmain", "acc"]
+SEMAPHORES = ["ldr", "ldw", "ldt", "ldu", "ldd", "vs", "cs", "evd", "carr", "arrn", "arrf", "rarr", "sent",
+              "ps", "fn", "ff", "strow", "stmain"]
 
 _PLAN = {}
 
@@ -62,19 +68,21 @@ def rank_program(g, core, T, topo):
         for (s, d, sslot, dslot, relay) in msgs:
             if relay == core:
                 _, n_in = _engines(topo, s, core, 1)
-                m, n = _engines(topo, core, d, 1)
+                m, n = _engines(topo, core, d, None)
                 rid, pid = topo.addr(d, core)
                 g.wait_ge(sem.rarr, n_in)
-                g.remote_dma(T.lnd[dslot], T.rb[:], sem.arr, sem.sent, pid, rid, m)
+                g.remote_dma(T.hb[:, 4 * dslot:4 * dslot + 1], T.rb[:], sem.arrf, sem.sent, pid, rid, m)
                 g.wait_ge(sem.sent, n)
         return
 
     add = AluOpType.add
     v = g.vector
-    peer = T.cores[rank ^ 1] if GC == 2 else None
+    peer = T.cores[rank ^ 1]
     mine = [mm for mm in msgs if mm[0] == core]
     far = [mm for mm in mine if mm[4] is not None]
     near = [mm for mm in mine if mm[4] is None]
+    in_far = [mm for mm in msgs if mm[1] == core and mm[4] is not None][0]
+    in_near = [mm for mm in msgs if mm[1] == core and mm[4] is None][0]
 
     g.sync.dma_start(T.sb[:], T.x[0:P:P - 1, :]).then_inc(sem.ldr, 16)
     g.scalar.dma_start(T.w[:, W:W + 2], T.x[:, 0:2]).then_inc(sem.ldt, 16)
@@ -96,10 +104,15 @@ def rank_program(g, core, T, topo):
     g.remote_dma(T.cb[:, :], T.w[:, W - 1:W + 1], sem.carr, sem.sent, pid, rid, m)
     sent += ncol
     for (s, d, sslot, dslot, relay) in near:
-        m, n = _engines(topo, core, d, 1, skip=1)
+        m, n = _engines(topo, core, d, None)
         rid, pid = topo.addr(d, core)
-        g.remote_dma(T.lnd[dslot], T.sb[sslot], sem.arr, sem.sent, pid, rid, m)
+        g.remote_dma(T.hb[:, 4 * dslot:4 * dslot + 1], T.sb[sslot], sem.arrn, sem.sent, pid, rid, m)
         sent += n
+
+    v.memset(T.one[0:1, 0:4], 1.0).then_inc(sem.cs, 1)
+    v.memset(T.ev[96:P, 0:4], 0.0).then_inc(sem.cs, 1)
+    g.scalar.wait_ge(sem.cs, 2)
+    g.scalar.dma_start(T.ev[P - 1:P, 0:1], T.one[0:1, 0:1]).then_inc(sem.evd, 16)
 
     nv = [0]
 
@@ -127,15 +140,32 @@ def rank_program(g, core, T, topo):
     done(v.tensor_tensor(T.s[:, 0:1], T.s[:, 0:1], T.cb[:, 0:1], add))
     done(v.tensor_tensor(T.s[:, W - 1:W], T.s[:, W - 1:W], T.cb[:, 1:2], add))
 
-    g.sync.wait_ge(sem.vs, nv[0])
     g.scalar.wait_ge(sem.vs, nv[0])
-    g.sync.dma_start(T.y[0:1, :], T.s[0:1, :]).then_inc(sem.strow, 16)
-    g.scalar.dma_start(T.y[P - 1:P, :], T.s[P - 1:P, :]).then_inc(sem.strow, 16)
-    g.sync.dma_start(T.y[1:P - 1, :], T.s[1:P - 1, :]).then_inc(sem.stmain, 16)
+    g.scalar.dma_start(T.y[1:P - 1, :], T.s[1:P - 1, :]).then_inc(sem.stmain, 16)
+
+    t = g.tensor
+    t.wait_ge(sem.vs, nv[0])
+    t.wait_ge(sem.cs, 2)
+    t.wait_ge(sem.evd, 16)
+    t.matmul(T.pt[:, 0:1], T.s[0:1, :], T.one[0:1, 0:1], True, True).then_inc(sem.ps, 1)
+    t.matmul(T.pt[:, BANK:BANK + 1], T.s[96:P, :], T.ev[96:P, 0:1], True, True).then_inc(sem.ps, 1)
+
+    _, n_near = _engines(topo, in_near[0], core, None)
+    _, n_far = _engines(topo, in_far[4], core, None)
+    jn, jf = in_near[3], in_far[3]
+    v.wait_ge(sem.ps, 2)
+    v.wait_ge(sem.arrn, n_near)
+    v.tensor_tensor(T.fc[:, 4 * jn:4 * jn + 1], T.pt[:, BANK * jn:BANK * jn + 1], T.hb[:, 4 * jn:4 * jn + 1],
+                    add).then_inc(sem.fn, 1)
+    v.wait_ge(sem.arrf, n_far)
+    v.tensor_tensor(T.fc[:, 4 * jf:4 * jf + 1], T.pt[:, BANK * jf:BANK * jf + 1], T.hb[:, 4 * jf:4 * jf + 1],
+                    add).then_inc(sem.ff, 1)
+    rown, rowf = jn * (P - 1), jf * (P - 1)
+    g.scalar.wait_ge(sem.fn, 1)
+    g.scalar.dma_start(T.y[rown:rown + 1, :], T.fc[:, 4 * jn:4 * jn + 1]).then_inc(sem.strow, 16)
+    g.sync.wait_ge(sem.ff, 1)
+    g.sync.dma_start(T.y[rowf:rowf + 1, :], T.fc[:, 4 * jf:4 * jf + 1]).then_inc(sem.strow, 16)
 
     g.wait_ge(sem.strow, 32)
-    g.wait_ge(sem.arr, 2)
-    g.dma_start(T.y[0:P:P - 1, :], T.lnd[:], accum_op=add).then_inc(sem.acc, 16)
-    g.wait_ge(sem.acc, 16)
     g.wait_ge(sem.stmain, 16)
     g.wait_ge(sem.sent, sent)

@@ -1,3 +1,4 @@
+from concourse.bass import DstId, RemoteDMATransfer
 from concourse.mybir import AluOpType
 
 GR, GC, P, W = 4, 2, 128, 128
@@ -5,114 +6,142 @@ HOSTS = 4
 BANK = 512
 
 SCRATCH = {
-    "sb":  ("dram", [2, P, 1], "float32"),
-    "rb":  ("dram", [P, 1], "float32"),
-    "hb":  ("sbuf", [P, 8], "float32"),
-    "fc":  ("sbuf", [P, 8], "float32"),
-    "w":   ("sbuf", [P, W + 2], "float32"),
+    "sbf": ("dram", [2, P, 1], "float32"),
+    "sbn": ("dram", [P, 1], "float32"),
+    "hz":  ("dram", [7 * P, 1], "float32"),
+    "lnd": ("dram", [P, 1], "float32"),
+    "zs":  ("sbuf", [P, W], "float32"),
+    "hb":  ("sbuf", [P, 4], "float32"),
+    "fc":  ("sbuf", [P, 4], "float32"),
+    "ce":  ("sbuf", [P, 4], "float32"),
+    "we":  ("sbuf", [P, W + 8], "float32"),
     "xu":  ("sbuf", [P, W], "float32"),
     "xd":  ("sbuf", [P, W], "float32"),
-    "q":   ("sbuf", [P, W], "float32"),
+    "q":   ("sbuf", [P, W + 4], "float32"),
     "s":   ("sbuf", [P, W], "float32"),
     "cb":  ("sbuf", [P, 2], "float32"),
     "one": ("sbuf", [P, 4], "float32"),
     "ev":  ("sbuf", [P, 4], "float32"),
-    "pt":  ("psum", [P, 2 * BANK], "float32"),
+    "pv":  ("psum", [P, BANK], "float32"),
+    "pt":  ("psum", [P, BANK], "float32"),
 }
-SEMAPHORES = ["ldr", "ldw", "ldt", "ldu", "ldd", "vs", "cs", "evd", "carr", "arrn", "arrf", "rarr", "sent",
-              "ps", "fn", "ff", "strow", "stmain"]
+SEMAPHORES = ["ldf", "ldn", "ldc", "ldw", "ldu", "ldd", "ldz", "ms", "zf", "evd", "vs", "carr", "harr", "arrn", "arrf",
+              "sent", "ps", "fn", "stf", "stn", "stmain"]
 
 _PLAN = {}
 
 
-def _engines(topo, src, dst, n, skip=0):
-    m = topo.mask(src, dst)
-    bits = [b for b in range(m.bit_length()) if (m >> b) & 1]
-    if n is None:
-        n = len(bits)
-    sel = bits[skip:skip + n]
-    return sum(1 << b for b in sel), len(sel)
+def _bits(m):
+    return [b for b in range(m.bit_length()) if (m >> b) & 1]
 
 
 def _plan(T, topo):
-    if "m" in _PLAN:
-        return _PLAN["m"]
+    if "p" in _PLAN:
+        return _PLAN["p"]
     cores = list(T.cores)
     world = range(HOSTS * topo.CORES_PER_HOST)
-    used = set()
-    msgs = []
-    for r, s in enumerate(cores):
+    plan = {}
+    taken = []
+    for r, d in enumerate(cores):
         gr, gc = divmod(r, GC)
-        for step, sslot, dslot in ((-1, 0, 1), (1, 1, 0)):
-            d = cores[((gr + step) % GR) * GC + gc]
-            relay = None
-            if not topo.may_write(s, d):
-                for c in world:
-                    if (c not in cores and c not in used and topo.chip(c) == topo.chip(s) == topo.chip(d)
-                            and topo.die(c) == topo.die(s) and topo.same_plane(s, c)
-                            and topo.may_write(s, c) and topo.may_write(c, d)):
-                        relay = c
-                        break
-                used.add(relay)
-            msgs.append((s, d, sslot, dslot, relay))
-    _PLAN["m"] = msgs
-    return msgs
+        up = cores[((gr - 1) % GR) * GC + gc]
+        dn = cores[((gr + 1) % GR) * GC + gc]
+        peer = cores[gr * GC + (gc + 1) % GC]
+        top = not topo.may_write(d, up)
+        far, near = (up, dn) if top else (dn, up)
+        cand = [c for c in world if c not in cores and c not in taken and topo.chip(c) == topo.chip(d)
+                and topo.die(c) == topo.die(d) and topo.may_write(c, d)
+                and all(topo.may_write(k, c) for k in (d, peer, far))]
+        busy = [topo.host(h) for h in taken]
+        cand.sort(key=lambda c: (busy.count(topo.host(c)), c))
+        taken.append(cand[0])
+        plan[d] = (top, far, near, peer, cand[0])
+    _PLAN["p"] = plan
+    return plan
+
+
+def _win(T, start):
+    return T.hz[start:start + P, :]
 
 
 def rank_program(g, core, T, topo):
-    msgs = _plan(T, topo)
+    plan = _plan(T, topo)
     sem = T.sem
-    rank = T.rank_of(core)
+    v = g.vector
+    NF = 2
 
-    if rank is None:
-        for (s, d, sslot, dslot, relay) in msgs:
-            if relay == core:
-                _, n_in = _engines(topo, s, core, 1)
-                m, n = _engines(topo, core, d, None)
-                rid, pid = topo.addr(d, core)
-                g.wait_ge(sem.rarr, n_in)
-                g.remote_dma(T.hb[:, 4 * dslot:4 * dslot + 1], T.rb[:], sem.arrf, sem.sent, pid, rid, m)
-                g.wait_ge(sem.sent, n)
+    if T.rank_of(core) is None:
+        for d in plan:
+            if plan[d][4] != core:
+                continue
+            v.memset(T.zs[0:1, :], 0.0).then_inc(sem.ms, 1)
+            g.sync.wait_ge(sem.ms, 1)
+            g.scalar.wait_ge(sem.ms, 1)
+            g.sync.dma_start(_win(T, 0), T.zs[0:1, :]).then_inc(sem.zf, 16)
+            g.scalar.dma_start(_win(T, 2 * P), T.zs[0:1, :]).then_inc(sem.zf, 16)
+            g.sync.dma_start(_win(T, 4 * P), T.zs[0:1, :]).then_inc(sem.zf, 16)
+            rid, pid = topo.addr(d, core)
+            fold = RemoteDMATransfer(
+                dst_ids=[DstId(rid=rid, pnc=pid)], dma_engine_mask=sum(1 << b for b in _bits(topo.mask(core, d))[0:NF]),
+                remote_sem=sem.arrf,
+                srcs=[_win(T, P), _win(T, P), _win(T, P - 1), _win(T, P + 1), _win(T, 4 * P - 1), _win(T, 2 * P + 1),
+                      _win(T, 5 * P), _win(T, 6 * P)],
+                dsts=[T.lnd[:]], alu_op=1)
+            g.wait_ge(sem.zf, 48)
+            g.wait_ge(sem.harr, 4)
+            g.remote_dma_fused([fold], local_sem=sem.sent)
+            g.wait_ge(sem.sent, NF)
         return
 
     add = AluOpType.add
-    v = g.vector
-    peer = T.cores[rank ^ 1]
-    mine = [mm for mm in msgs if mm[0] == core]
-    far = [mm for mm in mine if mm[4] is not None]
-    near = [mm for mm in mine if mm[4] is None]
-    in_far = [mm for mm in msgs if mm[1] == core and mm[4] is not None][0]
-    in_near = [mm for mm in msgs if mm[1] == core and mm[4] is None][0]
+    top, far, near, peer, helper = plan[core]
+    rf, rn = (0, P - 1) if top else (P - 1, 0)
+    sa, sn = (0, 1) if top else (1, 0)
 
-    g.sync.dma_start(T.sb[:], T.x[0:P:P - 1, :]).then_inc(sem.ldr, 16)
-    g.scalar.dma_start(T.w[:, W:W + 2], T.x[:, 0:2]).then_inc(sem.ldt, 16)
-    g.sync.dma_start(T.w[:, 0:W], T.x[:, :]).then_inc(sem.ldw, 16)
+    fills = [(T.zs[0:1, :], 0.0), (T.xu[0:1, :], 0.0), (T.we[:, 0:4], 0.0), (T.we[:, W + 4:W + 8], 0.0),
+             (T.one[0:1, 0:4], 1.0), (T.ev[96:P, 0:4], 0.0)]
+    for ap, val in fills:
+        v.memset(ap, val).then_inc(sem.ms, 1)
+    nm = len(fills)
+
+    r0 = 0 if top else P - 2
+    g.sync.dma_start(T.sbf[:], T.x[r0:r0 + 2, :]).then_inc(sem.ldf, 16)
+    g.scalar.dma_start(T.ce[:, 0:2], T.x[:, W - 2:W]).then_inc(sem.ldc, 16)
+    g.sync.dma_start(T.ce[:, 2:4], T.x[:, 0:2]).then_inc(sem.ldc, 16)
+    g.scalar.dma_start(T.sbn[:], T.x[rn:rn + 1, :]).then_inc(sem.ldn, 16)
+    g.sync.dma_start(T.we[:, 4:W + 4], T.x[:, :]).then_inc(sem.ldw, 16)
     g.scalar.dma_start(T.xu[1:P, :], T.x[0:P - 1, :]).then_inc(sem.ldu, 16)
     g.sync.dma_start(T.xd[0:P - 1, :], T.x[1:P, :]).then_inc(sem.ldd, 16)
-
-    sent = 0
-    g.wait_ge(sem.ldr, 16)
-    for (s, d, sslot, dslot, relay) in far:
-        m, n = _engines(topo, core, relay, 1)
-        rid, pid = topo.addr(relay, core)
-        g.remote_dma(T.rb[:], T.sb[sslot], sem.rarr, sem.sent, pid, rid, m)
-        sent += n
-    g.wait_ge(sem.ldw, 16)
-    g.wait_ge(sem.ldt, 16)
-    m, ncol = _engines(topo, core, peer, None)
-    rid, pid = topo.addr(peer, core)
-    g.remote_dma(T.cb[:, :], T.w[:, W - 1:W + 1], sem.carr, sem.sent, pid, rid, m)
-    sent += ncol
-    for (s, d, sslot, dslot, relay) in near:
-        m, n = _engines(topo, core, d, None)
-        rid, pid = topo.addr(d, core)
-        g.remote_dma(T.hb[:, 4 * dslot:4 * dslot + 1], T.sb[sslot], sem.arrn, sem.sent, pid, rid, m)
-        sent += n
-
-    v.memset(T.one[0:1, 0:4], 1.0).then_inc(sem.cs, 1)
-    v.memset(T.ev[96:P, 0:4], 0.0).then_inc(sem.cs, 1)
-    g.scalar.wait_ge(sem.cs, 2)
+    g.scalar.wait_ge(sem.ms, nm)
+    g.scalar.dma_start(T.xd[P - 1:P, :], T.zs[0:1, :]).then_inc(sem.ldz, 16)
     g.scalar.dma_start(T.ev[P - 1:P, 0:1], T.one[0:1, 0:1]).then_inc(sem.evd, 16)
+
+    to = ((helper, P), (plan[peer][4], 3 * P), (plan[far][4], 6 * P))
+    allowed = None
+    for h, _ in to:
+        allowed = topo.mask(core, h) if allowed is None else allowed & topo.mask(core, h)
+    allowed = _bits(allowed)
+    ids = [DstId(rid=topo.addr(h, core)[0], pnc=topo.addr(h, core)[1]) for h, _ in to]
+    calls = [RemoteDMATransfer(dst_ids=ids, dma_engine_mask=1 << allowed[0], remote_sem=sem.harr,
+                               srcs=[T.sbf[sa]], dsts=[_win(T, o) for _, o in to]),
+             RemoteDMATransfer(dst_ids=ids[0:1], dma_engine_mask=1 << allowed[1], remote_sem=sem.harr,
+                               srcs=[T.sbf[sn]], dsts=[_win(T, 5 * P)])]
+    g.wait_ge(sem.ldf, 16)
+    g.remote_dma_fused(calls, local_sem=sem.sent)
+    sent = 2
+
+    g.wait_ge(sem.ldc, 32)
+    m = topo.mask(core, peer)
+    ncol = len(_bits(m))
+    rid, pid = topo.addr(peer, core)
+    g.remote_dma(T.cb[:, :], T.ce[:, 1:3], sem.carr, sem.sent, pid, rid, m)
+    sent += ncol
+    g.wait_ge(sem.ldn, 16)
+    m = topo.mask(core, near)
+    nnear = len(_bits(m))
+    rid, pid = topo.addr(near, core)
+    g.remote_dma(T.hb[:, 0:1], T.sbn[:], sem.arrn, sem.sent, pid, rid, m)
+    sent += nnear
 
     nv = [0]
 
@@ -123,18 +152,17 @@ def rank_program(g, core, T, topo):
     def sync_v():
         v.wait_ge(sem.vs, nv[0])
 
-    done(v.memset(T.xu[0:1, :], 0.0))
+    v.wait_ge(sem.ms, nm)
     v.wait_ge(sem.ldw, 16)
-    done(v.tensor_tensor(T.q[:, 0:W - 1], T.w[:, 0:W - 1], T.w[:, 1:W], add))
-    sync_v()
-    done(v.tensor_tensor(T.s[:, 1:W - 1], T.q[:, 0:W - 2], T.q[:, 1:W - 1], add))
-    done(v.tensor_tensor(T.s[:, 0:1], T.q[:, 0:1], T.w[:, 0:1], add))
-    done(v.tensor_tensor(T.s[:, W - 1:W], T.q[:, W - 2:W - 1], T.w[:, W - 1:W], add))
+    done(v.tensor_tensor(T.q[:, 0:W + 1], T.we[:, 3:W + 4], T.we[:, 4:W + 5], add))
     v.wait_ge(sem.ldu, 16)
     v.wait_ge(sem.ldd, 16)
-    done(v.tensor_tensor(T.xu[0:P - 1, :], T.xu[0:P - 1, :], T.xd[0:P - 1, :], add))
+    v.wait_ge(sem.ldz, 16)
+    done(v.tensor_tensor(T.pv[:, 0:W], T.xu[:, :], T.xd[:, :], add))
     sync_v()
-    done(v.tensor_tensor(T.s[:, :], T.s[:, :], T.xu[:, :], add))
+    done(v.tensor_tensor(T.pv[:, 0:W], T.pv[:, 0:W], T.q[:, 0:W], add))
+    sync_v()
+    done(v.tensor_tensor(T.s[:, :], T.pv[:, 0:W], T.q[:, 1:W + 1], add))
     sync_v()
     v.wait_ge(sem.carr, ncol)
     done(v.tensor_tensor(T.s[:, 0:1], T.s[:, 0:1], T.cb[:, 0:1], add))
@@ -145,27 +173,22 @@ def rank_program(g, core, T, topo):
 
     t = g.tensor
     t.wait_ge(sem.vs, nv[0])
-    t.wait_ge(sem.cs, 2)
+    t.wait_ge(sem.ms, nm)
     t.wait_ge(sem.evd, 16)
-    t.matmul(T.pt[:, 0:1], T.s[0:1, :], T.one[0:1, 0:1], True, True).then_inc(sem.ps, 1)
-    t.matmul(T.pt[:, BANK:BANK + 1], T.s[96:P, :], T.ev[96:P, 0:1], True, True).then_inc(sem.ps, 1)
-
-    _, n_near = _engines(topo, in_near[0], core, None)
-    _, n_far = _engines(topo, in_far[4], core, None)
-    jn, jf = in_near[3], in_far[3]
-    v.wait_ge(sem.ps, 2)
-    v.wait_ge(sem.arrn, n_near)
-    v.tensor_tensor(T.fc[:, 4 * jn:4 * jn + 1], T.pt[:, BANK * jn:BANK * jn + 1], T.hb[:, 4 * jn:4 * jn + 1],
-                    add).then_inc(sem.fn, 1)
-    v.wait_ge(sem.arrf, n_far)
-    v.tensor_tensor(T.fc[:, 4 * jf:4 * jf + 1], T.pt[:, BANK * jf:BANK * jf + 1], T.hb[:, 4 * jf:4 * jf + 1],
-                    add).then_inc(sem.ff, 1)
-    rown, rowf = jn * (P - 1), jf * (P - 1)
+    if rn == 0:
+        t.matmul(T.pt[:, 0:1], T.s[0:1, :], T.one[0:1, 0:1], True, True).then_inc(sem.ps, 1)
+    else:
+        t.matmul(T.pt[:, 0:1], T.s[96:P, :], T.ev[96:P, 0:1], True, True).then_inc(sem.ps, 1)
+    v.wait_ge(sem.ps, 1)
+    v.wait_ge(sem.arrn, len(_bits(topo.mask(near, core))))
+    v.tensor_tensor(T.fc[:, 0:1], T.pt[:, 0:1], T.hb[:, 0:1], add).then_inc(sem.fn, 1)
     g.scalar.wait_ge(sem.fn, 1)
-    g.scalar.dma_start(T.y[rown:rown + 1, :], T.fc[:, 4 * jn:4 * jn + 1]).then_inc(sem.strow, 16)
-    g.sync.wait_ge(sem.ff, 1)
-    g.sync.dma_start(T.y[rowf:rowf + 1, :], T.fc[:, 4 * jf:4 * jf + 1]).then_inc(sem.strow, 16)
+    g.scalar.dma_start(T.y[rn:rn + 1, :], T.fc[:, 0:1]).then_inc(sem.stn, 16)
 
-    g.wait_ge(sem.strow, 32)
+    g.sync.wait_ge(sem.arrf, NF)
+    g.sync.dma_start(T.y[rf:rf + 1, :], T.lnd[:]).then_inc(sem.stf, 16)
+
+    g.wait_ge(sem.stf, 16)
+    g.wait_ge(sem.stn, 16)
     g.wait_ge(sem.stmain, 16)
     g.wait_ge(sem.sent, sent)

@@ -13,7 +13,6 @@ SCRATCH = {
     "zs":  ("sbuf", [P, W], "float32"),
     "hb":  ("sbuf", [P, 4], "float32"),
     "fc":  ("sbuf", [P, 4], "float32"),
-    "ce":  ("sbuf", [P, 4], "float32"),
     "we":  ("sbuf", [P, W + 8], "float32"),
     "xu":  ("sbuf", [P, W], "float32"),
     "xd":  ("sbuf", [P, W], "float32"),
@@ -25,7 +24,7 @@ SCRATCH = {
     "pv":  ("psum", [P, BANK], "float32"),
     "pt":  ("psum", [P, BANK], "float32"),
 }
-SEMAPHORES = ["ldf", "ldn", "ldc", "ldw", "ldu", "ldd", "ldz", "ms", "zf", "evd", "vs", "carr", "harr", "arrn", "arrf",
+SEMAPHORES = ["ldf", "ldn", "ldw", "ldu", "ldd", "ldz", "ms0", "ms", "zf", "evd", "vs", "carr", "harr", "arrn", "arrf",
               "sent", "ps", "fn", "stf", "stn", "stmain"]
 
 _PLAN = {}
@@ -33,6 +32,10 @@ _PLAN = {}
 
 def _bits(m):
     return [b for b in range(m.bit_length()) if (m >> b) & 1]
+
+
+def _mask(bits):
+    return sum(1 << b for b in bits)
 
 
 def _plan(T, topo):
@@ -60,6 +63,17 @@ def _plan(T, topo):
     return plan
 
 
+def _split(b):
+    return b[0:len(b) // 2], b[len(b) // 2:2 * (len(b) // 2)]
+
+
+def _halves(plan, topo, k):
+    m = None
+    for h in (plan[k][4], plan[plan[k][3]][4], plan[plan[k][1]][4]):
+        m = topo.mask(k, h) if m is None else m & topo.mask(k, h)
+    return _split(_bits(m))
+
+
 def _win(T, start):
     return T.hz[start:start + P, :]
 
@@ -68,7 +82,6 @@ def rank_program(g, core, T, topo):
     plan = _plan(T, topo)
     sem = T.sem
     v = g.vector
-    NF = 2
 
     if T.rank_of(core) is None:
         for d in plan:
@@ -81,16 +94,19 @@ def rank_program(g, core, T, topo):
             g.scalar.dma_start(_win(T, 2 * P), T.zs[0:1, :]).then_inc(sem.zf, 16)
             g.sync.dma_start(_win(T, 4 * P), T.zs[0:1, :]).then_inc(sem.zf, 16)
             rid, pid = topo.addr(d, core)
+            m = topo.mask(core, d)
             fold = RemoteDMATransfer(
-                dst_ids=[DstId(rid=rid, pnc=pid)], dma_engine_mask=sum(1 << b for b in _bits(topo.mask(core, d))[0:NF]),
-                remote_sem=sem.arrf,
-                srcs=[_win(T, P), _win(T, P), _win(T, P - 1), _win(T, P + 1), _win(T, 4 * P - 1), _win(T, 2 * P + 1),
-                      _win(T, 5 * P), _win(T, 6 * P)],
+                dst_ids=[DstId(rid=rid, pnc=pid)], dma_engine_mask=m, remote_sem=sem.arrf,
+                srcs=[_win(T, 5 * P), _win(T, P - 1), _win(T, P + 1), _win(T, 4 * P - 1), _win(T, 2 * P + 1),
+                      _win(T, 6 * P)],
                 dsts=[T.lnd[:]], alu_op=1)
+            expect = len(_halves(plan, topo, d)[1])
+            for k in (d, plan[d][3], plan[d][1]):
+                expect += len(_halves(plan, topo, k)[0])
             g.wait_ge(sem.zf, 48)
-            g.wait_ge(sem.harr, 4)
+            g.wait_ge(sem.harr, expect)
             g.remote_dma_fused([fold], local_sem=sem.sent)
-            g.wait_ge(sem.sent, NF)
+            g.wait_ge(sem.sent, len(_bits(m)))
         return
 
     add = AluOpType.add
@@ -98,50 +114,51 @@ def rank_program(g, core, T, topo):
     rf, rn = (0, P - 1) if top else (P - 1, 0)
     sa, sn = (0, 1) if top else (1, 0)
 
-    fills = [(T.zs[0:1, :], 0.0), (T.xu[0:1, :], 0.0), (T.we[:, 0:4], 0.0), (T.we[:, W + 4:W + 8], 0.0),
-             (T.one[0:1, 0:4], 1.0), (T.ev[96:P, 0:4], 0.0)]
+    first = [(T.zs[0:1, :], 0.0), (T.one[0:1, 0:4], 1.0), (T.ev[96:P, 0:4], 0.0)]
+    for ap, val in first:
+        v.memset(ap, val).then_inc(sem.ms0, 1)
+    fills = [(T.xu[0:1, :], 0.0), (T.we[:, 0:4], 0.0), (T.we[:, W + 4:W + 8], 0.0)]
     for ap, val in fills:
         v.memset(ap, val).then_inc(sem.ms, 1)
-    nm = len(fills)
+    n0, nm = len(first), len(fills)
 
     r0 = 0 if top else P - 2
     g.sync.dma_start(T.sbf[:], T.x[r0:r0 + 2, :]).then_inc(sem.ldf, 16)
-    g.scalar.dma_start(T.ce[:, 0:2], T.x[:, W - 2:W]).then_inc(sem.ldc, 16)
-    g.sync.dma_start(T.ce[:, 2:4], T.x[:, 0:2]).then_inc(sem.ldc, 16)
     g.scalar.dma_start(T.sbn[:], T.x[rn:rn + 1, :]).then_inc(sem.ldn, 16)
     g.sync.dma_start(T.we[:, 4:W + 4], T.x[:, :]).then_inc(sem.ldw, 16)
     g.scalar.dma_start(T.xu[1:P, :], T.x[0:P - 1, :]).then_inc(sem.ldu, 16)
     g.sync.dma_start(T.xd[0:P - 1, :], T.x[1:P, :]).then_inc(sem.ldd, 16)
-    g.scalar.wait_ge(sem.ms, nm)
+    g.scalar.wait_ge(sem.ms0, n0)
     g.scalar.dma_start(T.xd[P - 1:P, :], T.zs[0:1, :]).then_inc(sem.ldz, 16)
     g.scalar.dma_start(T.ev[P - 1:P, 0:1], T.one[0:1, 0:1]).then_inc(sem.evd, 16)
 
     to = ((helper, P), (plan[peer][4], 3 * P), (plan[far][4], 6 * P))
-    allowed = None
-    for h, _ in to:
-        allowed = topo.mask(core, h) if allowed is None else allowed & topo.mask(core, h)
-    allowed = _bits(allowed)
+    e1, e2 = _halves(plan, topo, core)
     ids = [DstId(rid=topo.addr(h, core)[0], pnc=topo.addr(h, core)[1]) for h, _ in to]
-    calls = [RemoteDMATransfer(dst_ids=ids, dma_engine_mask=1 << allowed[0], remote_sem=sem.harr,
+    calls = [RemoteDMATransfer(dst_ids=ids, dma_engine_mask=_mask(e1), remote_sem=sem.harr,
                                srcs=[T.sbf[sa]], dsts=[_win(T, o) for _, o in to]),
-             RemoteDMATransfer(dst_ids=ids[0:1], dma_engine_mask=1 << allowed[1], remote_sem=sem.harr,
-                               srcs=[T.sbf[sn]], dsts=[_win(T, 5 * P)])]
+             RemoteDMATransfer(dst_ids=ids[0:1], dma_engine_mask=_mask(e2), remote_sem=sem.harr,
+                               srcs=[T.sbf[sa], T.sbf[sa], T.sbf[sn]], dsts=[_win(T, 5 * P)], alu_op=1)]
     g.wait_ge(sem.ldf, 16)
     g.remote_dma_fused(calls, local_sem=sem.sent)
-    sent = 2
+    sent = len(e1) + len(e2)
 
-    g.wait_ge(sem.ldc, 32)
-    m = topo.mask(core, peer)
-    ncol = len(_bits(m))
+    c1, c2 = _split(_bits(topo.mask(core, peer)))
+    ncol = len(c1) + len(c2)
     rid, pid = topo.addr(peer, core)
-    g.remote_dma(T.cb[:, :], T.ce[:, 1:3], sem.carr, sem.sent, pid, rid, m)
+    pd = [DstId(rid=rid, pnc=pid)]
+    cols = [RemoteDMATransfer(dst_ids=pd, dma_engine_mask=_mask(c1), remote_sem=sem.carr,
+                              srcs=[T.we[:, W + 3:W + 4]], dsts=[T.cb[:, 0:1]]),
+            RemoteDMATransfer(dst_ids=pd, dma_engine_mask=_mask(c2), remote_sem=sem.carr,
+                              srcs=[T.we[:, 4:5]], dsts=[T.cb[:, 1:2]])]
+    g.wait_ge(sem.ldw, 16)
+    g.remote_dma_fused(cols, local_sem=sem.sent)
     sent += ncol
     g.wait_ge(sem.ldn, 16)
     m = topo.mask(core, near)
-    nnear = len(_bits(m))
     rid, pid = topo.addr(near, core)
     g.remote_dma(T.hb[:, 0:1], T.sbn[:], sem.arrn, sem.sent, pid, rid, m)
-    sent += nnear
+    sent += len(_bits(m))
 
     nv = [0]
 
@@ -173,7 +190,7 @@ def rank_program(g, core, T, topo):
 
     t = g.tensor
     t.wait_ge(sem.vs, nv[0])
-    t.wait_ge(sem.ms, nm)
+    t.wait_ge(sem.ms0, n0)
     t.wait_ge(sem.evd, 16)
     if rn == 0:
         t.matmul(T.pt[:, 0:1], T.s[0:1, :], T.one[0:1, 0:1], True, True).then_inc(sem.ps, 1)
@@ -185,7 +202,7 @@ def rank_program(g, core, T, topo):
     g.scalar.wait_ge(sem.fn, 1)
     g.scalar.dma_start(T.y[rn:rn + 1, :], T.fc[:, 0:1]).then_inc(sem.stn, 16)
 
-    g.sync.wait_ge(sem.arrf, NF)
+    g.sync.wait_ge(sem.arrf, len(_bits(topo.mask(helper, core))))
     g.sync.dma_start(T.y[rf:rf + 1, :], T.lnd[:]).then_inc(sem.stf, 16)
 
     g.wait_ge(sem.stf, 16)

from concourse.bass import DstId, RemoteDMATransfer
from concourse.mybir import AluOpType

GR, GC, P, W = 4, 2, 128, 128
HOSTS = 4
BANK = 512

SCRATCH = {
    "sbf": ("dram", [2, P, 1], "float32"),
    "sbn": ("dram", [P, 1], "float32"),
    "hz":  ("dram", [7 * P, 1], "float32"),
    "lnd": ("dram", [P, 1], "float32"),
    "zs":  ("sbuf", [P, W], "float32"),
    "hb":  ("sbuf", [P, 4], "float32"),
    "fc":  ("sbuf", [P, 4], "float32"),
    "we":  ("sbuf", [P, W + 8], "float32"),
    "xu":  ("sbuf", [P, W], "float32"),
    "xd":  ("sbuf", [P, W], "float32"),
    "q":   ("sbuf", [P, W + 4], "float32"),
    "s":   ("sbuf", [P, W], "float32"),
    "cb":  ("sbuf", [P, 2], "float32"),
    "one": ("sbuf", [P, 4], "float32"),
    "ev":  ("sbuf", [P, 4], "float32"),
    "pv":  ("psum", [P, BANK], "float32"),
    "pt":  ("psum", [P, BANK], "float32"),
}
SEMAPHORES = ["ldf", "ldn", "ldw", "ldu", "ldd", "ldz", "ms0", "ms", "zf", "evd", "vs", "carr", "harr", "arrn", "arrf",
              "sent", "ps", "fn", "stf", "stn", "stmain"]

_PLAN = {}


def _bits(m):
    return [b for b in range(m.bit_length()) if (m >> b) & 1]


def _mask(bits):
    return sum(1 << b for b in bits)


def _plan(T, topo):
    if "p" in _PLAN:
        return _PLAN["p"]
    cores = list(T.cores)
    world = range(HOSTS * topo.CORES_PER_HOST)
    plan = {}
    taken = []
    for r, d in enumerate(cores):
        gr, gc = divmod(r, GC)
        up = cores[((gr - 1) % GR) * GC + gc]
        dn = cores[((gr + 1) % GR) * GC + gc]
        peer = cores[gr * GC + (gc + 1) % GC]
        top = not topo.may_write(d, up)
        far, near = (up, dn) if top else (dn, up)
        cand = [c for c in world if c not in cores and c not in taken and topo.chip(c) == topo.chip(d)
                and topo.die(c) == topo.die(d) and topo.may_write(c, d)
                and all(topo.may_write(k, c) for k in (d, peer, far))]
        busy = [topo.host(h) for h in taken]
        cand.sort(key=lambda c: (busy.count(topo.host(c)), c))
        taken.append(cand[0])
        plan[d] = (top, far, near, peer, cand[0])
    _PLAN["p"] = plan
    return plan


def _split(b):
    return b[0:len(b) // 2], b[len(b) // 2:2 * (len(b) // 2)]


def _halves(plan, topo, k):
    m = None
    for h in (plan[k][4], plan[plan[k][3]][4], plan[plan[k][1]][4]):
        m = topo.mask(k, h) if m is None else m & topo.mask(k, h)
    return _split(_bits(m))


def _win(T, start):
    return T.hz[start:start + P, :]


def rank_program(g, core, T, topo):
    plan = _plan(T, topo)
    sem = T.sem
    v = g.vector

    if T.rank_of(core) is None:
        for d in plan:
            if plan[d][4] != core:
                continue
            v.memset(T.zs[0:1, :], 0.0).then_inc(sem.ms, 1)
            g.sync.wait_ge(sem.ms, 1)
            g.scalar.wait_ge(sem.ms, 1)
            g.sync.dma_start(_win(T, 0), T.zs[0:1, :]).then_inc(sem.zf, 16)
            g.scalar.dma_start(_win(T, 2 * P), T.zs[0:1, :]).then_inc(sem.zf, 16)
            g.sync.dma_start(_win(T, 4 * P), T.zs[0:1, :]).then_inc(sem.zf, 16)
            rid, pid = topo.addr(d, core)
            m = topo.mask(core, d)
            fold = RemoteDMATransfer(
                dst_ids=[DstId(rid=rid, pnc=pid)], dma_engine_mask=m, remote_sem=sem.arrf,
                srcs=[_win(T, 5 * P), _win(T, P - 1), _win(T, P + 1), _win(T, 4 * P - 1), _win(T, 2 * P + 1),
                      _win(T, 6 * P)],
                dsts=[T.lnd[:]], alu_op=1)
            expect = len(_halves(plan, topo, d)[1])
            for k in (d, plan[d][3], plan[d][1]):
                expect += len(_halves(plan, topo, k)[0])
            g.wait_ge(sem.zf, 48)
            g.wait_ge(sem.harr, expect)
            g.remote_dma_fused([fold], local_sem=sem.sent)
            g.wait_ge(sem.sent, len(_bits(m)))
        return

    add = AluOpType.add
    top, far, near, peer, helper = plan[core]
    rf, rn = (0, P - 1) if top else (P - 1, 0)
    sa, sn = (0, 1) if top else (1, 0)

    first = [(T.zs[0:1, :], 0.0), (T.one[0:1, 0:4], 1.0), (T.ev[96:P, 0:4], 0.0)]
    for ap, val in first:
        v.memset(ap, val).then_inc(sem.ms0, 1)
    fills = [(T.xu[0:1, :], 0.0), (T.we[:, 0:4], 0.0), (T.we[:, W + 4:W + 8], 0.0)]
    for ap, val in fills:
        v.memset(ap, val).then_inc(sem.ms, 1)
    n0, nm = len(first), len(fills)

    r0 = 0 if top else P - 2
    g.sync.dma_start(T.sbf[:], T.x[r0:r0 + 2, :]).then_inc(sem.ldf, 16)
    g.scalar.dma_start(T.sbn[:], T.x[rn:rn + 1, :]).then_inc(sem.ldn, 16)
    g.sync.dma_start(T.we[:, 4:W + 4], T.x[:, :]).then_inc(sem.ldw, 16)
    g.scalar.dma_start(T.xu[1:P, :], T.x[0:P - 1, :]).then_inc(sem.ldu, 16)
    g.sync.dma_start(T.xd[0:P - 1, :], T.x[1:P, :]).then_inc(sem.ldd, 16)
    g.scalar.wait_ge(sem.ms0, n0)
    g.scalar.dma_start(T.xd[P - 1:P, :], T.zs[0:1, :]).then_inc(sem.ldz, 16)
    g.scalar.dma_start(T.ev[P - 1:P, 0:1], T.one[0:1, 0:1]).then_inc(sem.evd, 16)

    to = ((helper, P), (plan[peer][4], 3 * P), (plan[far][4], 6 * P))
    e1, e2 = _halves(plan, topo, core)
    ids = [DstId(rid=topo.addr(h, core)[0], pnc=topo.addr(h, core)[1]) for h, _ in to]
    calls = [RemoteDMATransfer(dst_ids=ids, dma_engine_mask=_mask(e1), remote_sem=sem.harr,
                               srcs=[T.sbf[sa]], dsts=[_win(T, o) for _, o in to]),
             RemoteDMATransfer(dst_ids=ids[0:1], dma_engine_mask=_mask(e2), remote_sem=sem.harr,
                               srcs=[T.sbf[sa], T.sbf[sa], T.sbf[sn]], dsts=[_win(T, 5 * P)], alu_op=1)]
    g.wait_ge(sem.ldf, 16)
    g.remote_dma_fused(calls, local_sem=sem.sent)
    sent = len(e1) + len(e2)

    c1, c2 = _split(_bits(topo.mask(core, peer)))
    ncol = len(c1) + len(c2)
    rid, pid = topo.addr(peer, core)
    pd = [DstId(rid=rid, pnc=pid)]
    cols = [RemoteDMATransfer(dst_ids=pd, dma_engine_mask=_mask(c1), remote_sem=sem.carr,
                              srcs=[T.we[:, W + 3:W + 4]], dsts=[T.cb[:, 0:1]]),
            RemoteDMATransfer(dst_ids=pd, dma_engine_mask=_mask(c2), remote_sem=sem.carr,
                              srcs=[T.we[:, 4:5]], dsts=[T.cb[:, 1:2]])]
    g.wait_ge(sem.ldw, 16)
    g.remote_dma_fused(cols, local_sem=sem.sent)
    sent += ncol
    g.wait_ge(sem.ldn, 16)
    m = topo.mask(core, near)
    rid, pid = topo.addr(near, core)
    g.remote_dma(T.hb[:, 0:1], T.sbn[:], sem.arrn, sem.sent, pid, rid, m)
    sent += len(_bits(m))

    nv = [0]

    def done(inst):
        inst.then_inc(sem.vs, 1)
        nv[0] += 1

    def sync_v():
        v.wait_ge(sem.vs, nv[0])

    v.wait_ge(sem.ms, nm)
    v.wait_ge(sem.ldw, 16)
    done(v.tensor_tensor(T.q[:, 0:W + 1], T.we[:, 3:W + 4], T.we[:, 4:W + 5], add))
    v.wait_ge(sem.ldu, 16)
    v.wait_ge(sem.ldd, 16)
    v.wait_ge(sem.ldz, 16)
    done(v.tensor_tensor(T.pv[:, 0:W], T.xu[:, :], T.xd[:, :], add))
    sync_v()
    done(v.tensor_tensor(T.pv[:, 0:W], T.pv[:, 0:W], T.q[:, 0:W], add))
    sync_v()
    done(v.tensor_tensor(T.s[:, :], T.pv[:, 0:W], T.q[:, 1:W + 1], add))
    sync_v()
    v.wait_ge(sem.carr, ncol)
    done(v.tensor_tensor(T.s[:, 0:1], T.s[:, 0:1], T.cb[:, 0:1], add))
    done(v.tensor_tensor(T.s[:, W - 1:W], T.s[:, W - 1:W], T.cb[:, 1:2], add))

    g.scalar.wait_ge(sem.vs, nv[0])
    g.scalar.dma_start(T.y[1:P - 1, :], T.s[1:P - 1, :]).then_inc(sem.stmain, 16)

    t = g.tensor
    t.wait_ge(sem.vs, nv[0])
    t.wait_ge(sem.ms0, n0)
    t.wait_ge(sem.evd, 16)
    if rn == 0:
        t.matmul(T.pt[:, 0:1], T.s[0:1, :], T.one[0:1, 0:1], True, True).then_inc(sem.ps, 1)
    else:
        t.matmul(T.pt[:, 0:1], T.s[96:P, :], T.ev[96:P, 0:1], True, True).then_inc(sem.ps, 1)
    v.wait_ge(sem.ps, 1)
    v.wait_ge(sem.arrn, len(_bits(topo.mask(near, core))))
    v.tensor_tensor(T.fc[:, 0:1], T.pt[:, 0:1], T.hb[:, 0:1], add).then_inc(sem.fn, 1)
    g.scalar.wait_ge(sem.fn, 1)
    g.scalar.dma_start(T.y[rn:rn + 1, :], T.fc[:, 0:1]).then_inc(sem.stn, 16)

    g.sync.wait_ge(sem.arrf, len(_bits(topo.mask(helper, core))))
    g.sync.dma_start(T.y[rf:rf + 1, :], T.lnd[:]).then_inc(sem.stf, 16)

    g.wait_ge(sem.stf, 16)
    g.wait_ge(sem.stn, 16)
    g.wait_ge(sem.stmain, 16)
    g.wait_ge(sem.sent, sent)
